import numpy as np
import ml_dtypes


def mxq(x, axis, fmt="e4m3"):
    dtype, down = {"e4m3": (ml_dtypes.float8_e4m3fn, 7), "e5m2": (ml_dtypes.float8_e5m2, 14)}[fmt]
    v = np.moveaxis(np.asarray(x, np.float32).astype(ml_dtypes.bfloat16).astype(np.float64), axis, -1)
    blocks = v.reshape(v.shape[:-1] + (-1, 32))
    amax = np.abs(blocks).max(-1, keepdims=True)
    byte = np.maximum(np.where(amax > 0, np.frexp(amax)[1] - 1 + 127, 0) - down, 1)
    scale = np.exp2(byte - 127.0)
    codes = (blocks / scale).astype(np.float32).astype(dtype).astype(np.float64)
    return np.moveaxis((codes * scale).reshape(v.shape), -1, axis)


WIDE = False


def mx_kscale(k):
    if not WIDE:
        return np.ones(k)
    levels = np.array([10, -10, 5, -5, 0])
    if k % 512:
        return np.exp2(np.random.permutation(np.resize(levels, k // 32))).repeat(32)
    a = np.empty((k // 512, 16))
    for p in range(k // 512):
        a[p, :8] = np.random.permutation(np.resize(levels, 8))
        for g in range(8):
            far = levels[np.abs(levels - a[p, g]) >= 10]
            a[p, g + 8] = far[np.random.randint(len(far))]
    return np.exp2(a.ravel()).repeat(32)


def f64(x):
    return np.asarray(x).astype(np.float64)


def striped(idx):
    return np.tile(idx.reshape(-1, 16).T, (8, 1)).astype(np.uint16)


def unstriped(offs):
    return offs[:16].T.reshape(-1).astype(np.int64)


def sigmoid(v):
    return 1.0 / (1.0 + np.exp(-np.maximum(v, -700.0)))


K, T, S, H, N = 512, 4096, 1536, 1024, 128


def setup_inputs():
    n = np.random.standard_normal
    s = mx_kscale(K)[:, None]
    u = mx_kscale(H)
    return {
        "xT": (n((K, T)) * s).astype(np.float32),
        "w1": (n((K, H)) / np.sqrt(K) / s).astype(np.float32),
        "w3": (n((K, H)) / np.sqrt(K) / s * u).astype(np.float32),
        "w2": (n((H, N)) / np.sqrt(H) / u[:, None]).astype(np.float32),
        "offs": striped(np.random.permutation(T)[:S]),
    }


def reference(xT, w1, w3, w2, offs):
    idx = unstriped(offs)
    xq = mxq(f64(xT)[:, idx], 0, "e4m3")
    h = sigmoid(mxq(f64(w1), 0, "e4m3").T @ xq) * (mxq(f64(w3), 0, "e4m3").T @ xq)
    y = mxq(f64(w2), 0, "e4m3").T @ mxq(h, 0, "e4m3")
    return y

@@ -1,0 +1,229 @@
+from contextlib import ExitStack
+
+import concourse.mybir as mybir
+
+K, T, S, H, N = 512, 4096, 1536, 1024, 128
+FLOPS = 2 * S * (2 * K * H + H * N)
+
+P = 128
+PACK = 4
+F32 = mybir.dt.float32
+BF16 = mybir.dt.bfloat16
+U32 = mybir.dt.uint32
+U16 = mybir.dt.uint16
+U8 = mybir.dt.uint8
+FP8X4 = mybir.dt.float8_e4m3fn_x4
+Copy = mybir.ActivationFunctionType.Copy
+Sigmoid = mybir.ActivationFunctionType.Sigmoid
+mult = mybir.AluOpType.mult
+add = mybir.AluOpType.add
+
+CHUNK = 1024
+SLICE = 512
+GROUP = 128
+ON_GPSIMD = ()
+HALF = 512
+
+
+def tile_picked_pick_glu_sigmoid_sub_e_kernel(tc, xT, w1, w3, w2, offs, out):
+    nc = tc.nc
+    slices = S // SLICE
+    halves = H // HALF
+    with ExitStack() as ctx:
+        keep = ctx.enter_context(tc.tile_pool(name="keep", bufs=1))
+        stage = ctx.enter_context(tc.tile_pool(name="stage", bufs=8))
+        work = ctx.enter_context(tc.tile_pool(name="work", bufs=4))
+        res = ctx.enter_context(tc.tile_pool(name="res", bufs=3))
+        psum_h = ctx.enter_context(tc.psum_pool(name="psum_h", bufs=3))
+        psum_y = ctx.enter_context(tc.psum_pool(name="psum_y", bufs=2))
+
+        offsets = keep.tile([P, S // 16], U16, name="offsets")
+        nc.sync.dma_start(offsets[:], offs)
+
+        warm = keep.tile([P, 8], F32, name="warm")
+        nc.vector.memset(warm[:], 0.0)
+        nc.scalar.activation(warm[:, 0:1], warm[:, 0:1], Sigmoid)
+
+        x_rows = xT.rearrange("(p j) t -> p j t", j=PACK)
+        pairs = [keep.tile([P, 2 * T], BF16, align_bytes=64, name=f"pairs{u}") for u in range(2)]
+        picked = [keep.tile([P, SLICE * PACK], BF16, align_bytes=64, name=f"picked{s}") for s in range(slices)]
+        x_codes = [keep.tile([P, SLICE], U32, align_bytes=64, name=f"x_codes{s}") for s in range(slices)]
+        x_scales = [keep.tile([P, SLICE], U8, align_bytes=64, name=f"x_scales{s}") for s in range(slices)]
+
+        def load_x(u, t0, width, engines):
+            raw = stage.tile([P, 2, width], F32, name="raw")
+            nc.sync.dma_start(out=raw[:], in_=x_rows[:, 2 * u : 2 * u + 2, t0 : t0 + width])
+            part = width // len(engines)
+            for i, engine in enumerate(engines):
+                a = t0 + i * part
+                dst = pairs[u][:, 2 * a : 2 * (a + part)].rearrange("p (t e) -> p t e", e=2)
+                src = raw[:, :, i * part : (i + 1) * part].rearrange("p e t -> p t e")
+                if engine == "V":
+                    nc.vector.tensor_copy(dst, src)
+                else:
+                    nc.scalar.activation(dst, src, Copy)
+
+        def gather(u, s):
+            words = picked[s][:].bitcast(U32).rearrange("p (n u) -> p n u", u=2)
+            window = pairs[u][:].bitcast(U32)
+            cols = offsets[:, s * (SLICE // 16) : (s + 1) * (SLICE // 16)]
+            nc.vector.tensor_copy(words[:, :, u], window.indirect(cols))
+
+        for i in range(4):
+            load_x(0, i * CHUNK, CHUNK, "SV"[i % 2])
+        load_x(1, 0, CHUNK, "S")
+        gather(0, 0)
+        load_x(1, CHUNK, CHUNK, "V")
+        gather(0, 1)
+        load_x(1, 2 * CHUNK, CHUNK, "S")
+        gather(0, 2)
+        load_x(1, 3 * CHUNK, CHUNK // 2, "V")
+        load_x(1, 3 * CHUNK + CHUNK // 2, CHUNK // 2, "VS")
+
+        w_codes = {}
+        w_scales = {}
+
+        def load_w(name, w, h, engines):
+            raw = stage.tile([P, PACK, HALF], F32, name="raw")
+            rows = w.rearrange("(p j) c -> p j c", j=PACK)
+            nc.sync.dma_start(out=raw[:], in_=rows[:, :, h * HALF : (h + 1) * HALF])
+            grouped = keep.tile([P, HALF * PACK], BF16, align_bytes=64, name=f"{name}_grouped{h}")
+            src = raw[:].rearrange("p j (q t r) -> p t q r j", t=PACK, r=8)
+            dst = grouped[:].rearrange("p (t q r j) -> p t q r j", t=PACK, r=8, j=PACK)
+            for t, engine in enumerate(engines):
+                if engine == "S":
+                    nc.scalar.activation(dst[:, t], src[:, t], Copy)
+                elif engine == "V":
+                    nc.vector.tensor_copy(dst[:, t], src[:, t])
+                else:
+                    nc.gpsimd.tensor_scalar(dst[:, t], src[:, t], 1.0, 0.0, mult, add)
+            return grouped
+
+        def quantize_w(name, h, grouped):
+            codes = keep.tile([P, HALF], U32, align_bytes=64, name=f"{name}_codes{h}")
+            scales = keep.tile([P, HALF], U8, align_bytes=64, name=f"{name}_scales{h}")
+            nc.vector.quantize_mx(out=codes[:].bitcast(FP8X4), scales=scales[:], in_=grouped[:])
+            w_codes[name, h] = codes
+            w_scales[name, h] = scales
+
+        def quantize_x(s):
+            nc.vector.quantize_mx(out=x_codes[s][:].bitcast(FP8X4), scales=x_scales[s][:], in_=picked[s][:])
+
+        gather(1, 0)
+        w1a = load_w("w1", w1, 0, "SGSG")
+        w3a = load_w("w3", w3, 0, "SGSG")
+        quantize_x(0)
+        quantize_w("w1", 0, w1a)
+        quantize_w("w3", 0, w3a)
+
+        later = []
+
+        def load_b():
+            later.append(load_w("w1", w1, 1, "GGGG"))
+            later.append(load_w("w3", w3, 1, "GGGG"))
+
+        w2_raw = keep.tile([P, halves, PACK, N], F32, name="w2_raw")
+        w2_grouped = keep.tile([P, halves * N * PACK], BF16, align_bytes=64, name="w2_grouped")
+        w2_codes = keep.tile([P, halves * N], U32, align_bytes=64, name="w2_codes")
+        w2_scales = keep.tile([P, halves * N], U8, align_bytes=64, name="w2_scales")
+        w2_rows = w2.rearrange("(g q t r) m -> g t q r m", g=halves, t=PACK, r=8)
+
+        def load_w2():
+            for g in range(halves):
+                for t in range(PACK):
+                    nc.sync.dma_start(out=w2_raw[:, g, t, :], in_=w2_rows[g, t])
+            for g in range(halves):
+                nc.gpsimd.tensor_scalar(
+                    w2_grouped[:, g * N * PACK : (g + 1) * N * PACK].rearrange("p (m t) -> p m t", t=PACK),
+                    w2_raw[:, g].rearrange("p t m -> p m t"),
+                    1.0, 0.0, mult, add,
+                )
+            nc.vector.quantize_mx(out=w2_codes[:].bitcast(FP8X4), scales=w2_scales[:], in_=w2_grouped[:])
+
+        h_codes = {}
+        h_scales = {}
+        for h in range(halves):
+            for s in range(slices):
+                hidden = work.tile([P, SLICE * PACK], BF16, align_bytes=64, name="hidden")
+                codes = keep.tile([P, SLICE], U32, align_bytes=64, name=f"h_codes{h}_{s}")
+                scales = keep.tile([P, SLICE], U8, align_bytes=64, name=f"h_scales{h}_{s}")
+                last = h == halves - 1 and s == slices - 1
+                step = 2 * GROUP if last else SLICE
+                for c in range(SLICE // GROUP):
+                    n_cols = slice(c * GROUP, (c + 1) * GROUP)
+                    banks = []
+                    for name in ("w1", "w3"):
+                        bank = psum_h.tile([P, PACK * GROUP], F32, name=f"{name}_bank")
+                        for t in range(PACK):
+                            m_cols = slice(t * P, (t + 1) * P)
+                            nc.tensor.matmul_mx(
+                                out=bank[:, t * GROUP : (t + 1) * GROUP],
+                                lhsT=w_codes[name, h][:, m_cols].bitcast(FP8X4),
+                                lhsT_scale=w_scales[name, h][:, m_cols],
+                                rhs=x_codes[s][:, n_cols].bitcast(FP8X4),
+                                rhs_scale=x_scales[s][:, n_cols],
+                                start=True,
+                                stop=True,
+                            )
+                        banks.append(bank)
+                    gate = work.tile([P, GROUP * PACK], F32, name="gate")
+                    nc.scalar.activation(
+                        gate[:].rearrange("p (n t) -> p n t", t=PACK),
+                        banks[0][:].rearrange("p (t n) -> p n t", t=PACK),
+                        Sigmoid,
+                    )
+                    into = hidden[:, c * GROUP * PACK : (c + 1) * GROUP * PACK]
+                    if (h, s, c) in ON_GPSIMD:
+                        value = work.tile([P, GROUP * PACK], F32, name="value")
+                        nc.scalar.activation(
+                            value[:].rearrange("p (n t) -> p n t", t=PACK),
+                            banks[1][:].rearrange("p (t n) -> p n t", t=PACK),
+                            Copy,
+                        )
+                        nc.gpsimd.tensor_tensor(into, value[:], gate[:], mult)
+                    else:
+                        nc.vector.tensor_tensor(
+                            into.rearrange("p (n t) -> p n t", t=PACK),
+                            banks[1][:].rearrange("p (t n) -> p n t", t=PACK),
+                            gate[:].rearrange("p (n t) -> p n t", t=PACK),
+                            mult,
+                        )
+                    if (h, s, c) == (0, 0, 0):
+                        gather(1, 1)
+                    if (h, s, c) == (0, 0, 1):
+                        quantize_x(1)
+                        gather(1, 2)
+                    if (h, s, c) == (0, 0, 2):
+                        quantize_x(2)
+                        load_b()
+                    if (h, s, c) == (0, 1, 1):
+                        quantize_w("w1", 1, later[0])
+                        quantize_w("w3", 1, later[1])
+                        load_w2()
+                    done = (c + 1) * GROUP
+                    if done % step == 0:
+                        q = slice(done - step, done)
+                        nc.vector.quantize_mx(
+                            out=codes[:, q].bitcast(FP8X4),
+                            scales=scales[:, q],
+                            in_=hidden[:, (done - step) * PACK : done * PACK],
+                        )
+                h_codes[h, s] = codes
+                h_scales[h, s] = scales
+                if h == halves - 1:
+                    for n0 in range(0, SLICE, step):
+                        n_cols = slice(n0, n0 + step)
+                        acc = psum_y.tile([P, step], F32, name="acc")
+                        for g in range(halves):
+                            nc.tensor.matmul_mx(
+                                out=acc[:],
+                                lhsT=w2_codes[:, g * N : (g + 1) * N].bitcast(FP8X4),
+                                lhsT_scale=w2_scales[:, g * N : (g + 1) * N],
+                                rhs=h_codes[g, s][:, n_cols].bitcast(FP8X4),
+                                rhs_scale=h_scales[g, s][:, n_cols],
+                                start=(g == 0),
+                                stop=(g == halves - 1),
+                            )
+                        y = res.tile([P, step], F32, name="y")
+                        nc.scalar.copy(y[:], acc[:])
+                        nc.sync.dma_start(out=out[:, s * SLICE + n0 : s * SLICE + n0 + step], in_=y[:])

@@ -1,4 +1,5 @@
 from contextlib import ExitStack
+from functools import partial
 
 import concourse.mybir as mybir
 
@@ -21,7 +22,7 @@ add = mybir.AluOpType.add
 CHUNK = 1024
 SLICE = 512
 GROUP = 128
-ON_GPSIMD = ()
+ON_GPSIMD = ((0, 0, 1), (0, 1, 1), (0, 2, 1), (1, 0, 1), (1, 1, 1))
 HALF = 512
 
 
@@ -34,7 +35,8 @@ def tile_picked_pick_glu_sigmoid_sub_e_kernel(tc, xT, w1, w3, w2, offs, out):
         stage = ctx.enter_context(tc.tile_pool(name="stage", bufs=8))
         work = ctx.enter_context(tc.tile_pool(name="work", bufs=4))
         res = ctx.enter_context(tc.tile_pool(name="res", bufs=3))
-        psum_h = ctx.enter_context(tc.psum_pool(name="psum_h", bufs=3))
+        psum_1 = ctx.enter_context(tc.psum_pool(name="psum_1", bufs=2))
+        psum_3 = ctx.enter_context(tc.psum_pool(name="psum_3", bufs=4))
         psum_y = ctx.enter_context(tc.psum_pool(name="psum_y", bufs=2))
 
         offsets = keep.tile([P, S // 16], U16, name="offsets")
@@ -110,7 +112,7 @@ def tile_picked_pick_glu_sigmoid_sub_e_kernel(tc, xT, w1, w3, w2, offs, out):
             nc.vector.quantize_mx(out=x_codes[s][:].bitcast(FP8X4), scales=x_scales[s][:], in_=picked[s][:])
 
         gather(1, 0)
-        w1a = load_w("w1", w1, 0, "SGSG")
+        w1a = load_w("w1", w1, 0, "SSSS")
         w3a = load_w("w3", w3, 0, "SGSG")
         quantize_x(0)
         quantize_w("w1", 0, w1a)
@@ -142,18 +144,47 @@ def tile_picked_pick_glu_sigmoid_sub_e_kernel(tc, xT, w1, w3, w2, offs, out):
 
         h_codes = {}
         h_scales = {}
+        pending = []
+
+        def finish(h, s, hidden, start, done):
+            n_cols = slice(start, done)
+            nc.vector.quantize_mx(
+                out=h_codes[h, s][:, n_cols].bitcast(FP8X4),
+                scales=h_scales[h, s][:, n_cols],
+                in_=hidden[:, start * PACK : done * PACK],
+            )
+            if h < halves - 1:
+                return
+            acc = psum_y.tile([P, done - start], F32, name="acc")
+            for g in range(halves):
+                nc.tensor.matmul_mx(
+                    out=acc[:],
+                    lhsT=w2_codes[:, g * N : (g + 1) * N].bitcast(FP8X4),
+                    lhsT_scale=w2_scales[:, g * N : (g + 1) * N],
+                    rhs=h_codes[g, s][:, n_cols].bitcast(FP8X4),
+                    rhs_scale=h_scales[g, s][:, n_cols],
+                    start=(g == 0),
+                    stop=(g == halves - 1),
+                )
+            y = res.tile([P, done - start], F32, name="y")
+            nc.scalar.copy(y[:], acc[:])
+            nc.sync.dma_start(out=out[:, s * SLICE + start : s * SLICE + done], in_=y[:])
+
         for h in range(halves):
             for s in range(slices):
                 hidden = work.tile([P, SLICE * PACK], BF16, align_bytes=64, name="hidden")
                 codes = keep.tile([P, SLICE], U32, align_bytes=64, name=f"h_codes{h}_{s}")
                 scales = keep.tile([P, SLICE], U8, align_bytes=64, name=f"h_scales{h}_{s}")
+                h_codes[h, s] = codes
+                h_scales[h, s] = scales
                 last = h == halves - 1 and s == slices - 1
-                step = 2 * GROUP if last else SLICE
+                ends = [256, 384, 512] if last else [SLICE]
                 for c in range(SLICE // GROUP):
                     n_cols = slice(c * GROUP, (c + 1) * GROUP)
                     banks = []
                     for name in ("w1", "w3"):
-                        bank = psum_h.tile([P, PACK * GROUP], F32, name=f"{name}_bank")
+                        pool = psum_1 if name == "w1" else psum_3
+                        bank = pool.tile([P, PACK * GROUP], F32, name=f"{name}_bank")
                         for t in range(PACK):
                             m_cols = slice(t * P, (t + 1) * P)
                             nc.tensor.matmul_mx(
@@ -180,7 +211,8 @@ def tile_picked_pick_glu_sigmoid_sub_e_kernel(tc, xT, w1, w3, w2, offs, out):
                             banks[1][:].rearrange("p (t n) -> p n t", t=PACK),
                             Copy,
                         )
-                        nc.gpsimd.tensor_tensor(into, value[:], gate[:], mult)
+                        for a in (0, 256):
+                            nc.gpsimd.tensor_tensor(into[:, a : a + 256], value[:, a : a + 256], gate[:, a : a + 256], mult)
                     else:
                         nc.vector.tensor_tensor(
                             into.rearrange("p (n t) -> p n t", t=PACK),
@@ -188,42 +220,25 @@ def tile_picked_pick_glu_sigmoid_sub_e_kernel(tc, xT, w1, w3, w2, offs, out):
                             gate[:].rearrange("p (n t) -> p n t", t=PACK),
                             mult,
                         )
+                        for job in pending:
+                            job()
+                        pending.clear()
                     if (h, s, c) == (0, 0, 0):
                         gather(1, 1)
                     if (h, s, c) == (0, 0, 1):
-                        quantize_x(1)
                         gather(1, 2)
+                        quantize_x(1)
                     if (h, s, c) == (0, 0, 2):
                         quantize_x(2)
                         load_b()
-                    if (h, s, c) == (0, 1, 1):
+                    if (h, s, c) == (0, 2, 0):
                         quantize_w("w1", 1, later[0])
+                    if (h, s, c) == (0, 2, 2):
                         quantize_w("w3", 1, later[1])
                         load_w2()
                     done = (c + 1) * GROUP
-                    if done % step == 0:
-                        q = slice(done - step, done)
-                        nc.vector.quantize_mx(
-                            out=codes[:, q].bitcast(FP8X4),
-                            scales=scales[:, q],
-                            in_=hidden[:, (done - step) * PACK : done * PACK],
-                        )
-                h_codes[h, s] = codes
-                h_scales[h, s] = scales
-                if h == halves - 1:
-                    for n0 in range(0, SLICE, step):
-                        n_cols = slice(n0, n0 + step)
-                        acc = psum_y.tile([P, step], F32, name="acc")
-                        for g in range(halves):
-                            nc.tensor.matmul_mx(
-                                out=acc[:],
-                                lhsT=w2_codes[:, g * N : (g + 1) * N].bitcast(FP8X4),
-                                lhsT_scale=w2_scales[:, g * N : (g + 1) * N],
-                                rhs=h_codes[g, s][:, n_cols].bitcast(FP8X4),
-                                rhs_scale=h_scales[g, s][:, n_cols],
-                                start=(g == 0),
-                                stop=(g == halves - 1),
-                            )
-                        y = res.tile([P, step], F32, name="y")
-                        nc.scalar.copy(y[:], acc[:])
-                        nc.sync.dma_start(out=out[:, s * SLICE + n0 : s * SLICE + n0 + step], in_=y[:])
+                    if done in ends:
+                        start = ([0] + ends)[ends.index(done)]
+                        pending.append(partial(finish, h, s, hidden, start, done))
+        for job in pending:
+            job()

@@ -22,7 +22,6 @@ add = mybir.AluOpType.add
 CHUNK = 1024
 SLICE = 512
 GROUP = 128
-ON_GPSIMD = ((0, 0, 1), (0, 1, 1), (0, 2, 1), (1, 0, 1), (1, 1, 1))
 HALF = 512
 
 
@@ -35,9 +34,8 @@ def tile_picked_pick_glu_sigmoid_sub_e_kernel(tc, xT, w1, w3, w2, offs, out):
         stage = ctx.enter_context(tc.tile_pool(name="stage", bufs=8))
         work = ctx.enter_context(tc.tile_pool(name="work", bufs=4))
         res = ctx.enter_context(tc.tile_pool(name="res", bufs=3))
-        psum_1 = ctx.enter_context(tc.psum_pool(name="psum_1", bufs=2))
+        psum_1 = ctx.enter_context(tc.psum_pool(name="psum_1", bufs=4))
         psum_3 = ctx.enter_context(tc.psum_pool(name="psum_3", bufs=4))
-        psum_y = ctx.enter_context(tc.psum_pool(name="psum_y", bufs=2))
 
         offsets = keep.tile([P, S // 16], U16, name="offsets")
         nc.sync.dma_start(offsets[:], offs)
@@ -79,8 +77,8 @@ def tile_picked_pick_glu_sigmoid_sub_e_kernel(tc, xT, w1, w3, w2, offs, out):
         gather(0, 1)
         load_x(1, 2 * CHUNK, CHUNK, "S")
         gather(0, 2)
-        load_x(1, 3 * CHUNK, CHUNK // 2, "V")
-        load_x(1, 3 * CHUNK + CHUNK // 2, CHUNK // 2, "VS")
+        load_x(1, 3 * CHUNK, CHUNK // 2, "VS")
+        load_x(1, 3 * CHUNK + CHUNK // 2, CHUNK // 2, "V")
 
         w_codes = {}
         w_scales = {}
@@ -112,11 +110,15 @@ def tile_picked_pick_glu_sigmoid_sub_e_kernel(tc, xT, w1, w3, w2, offs, out):
             nc.vector.quantize_mx(out=x_codes[s][:].bitcast(FP8X4), scales=x_scales[s][:], in_=picked[s][:])
 
         gather(1, 0)
-        w1a = load_w("w1", w1, 0, "SSSS")
-        w3a = load_w("w3", w3, 0, "SGSG")
+        gather(1, 1)
         quantize_x(0)
-        quantize_w("w1", 0, w1a)
+        gather(1, 2)
+        quantize_x(1)
+        w3a = load_w("w3", w3, 0, "SGSG")
+        w1a = load_w("w1", w1, 0, "SGSG")
         quantize_w("w3", 0, w3a)
+        quantize_x(2)
+        quantize_w("w1", 0, w1a)
 
         later = []
 
@@ -155,7 +157,7 @@ def tile_picked_pick_glu_sigmoid_sub_e_kernel(tc, xT, w1, w3, w2, offs, out):
             )
             if h < halves - 1:
                 return
-            acc = psum_y.tile([P, done - start], F32, name="acc")
+            acc = psum_1.tile([P, done - start], F32, name="acc", tag="w1_bank")
             for g in range(halves):
                 nc.tensor.matmul_mx(
                     out=acc[:],
@@ -178,13 +180,13 @@ def tile_picked_pick_glu_sigmoid_sub_e_kernel(tc, xT, w1, w3, w2, offs, out):
                 h_codes[h, s] = codes
                 h_scales[h, s] = scales
                 last = h == halves - 1 and s == slices - 1
-                ends = [256, 384, 512] if last else [SLICE]
+                ends = [256, 512] if last else [SLICE]
                 for c in range(SLICE // GROUP):
                     n_cols = slice(c * GROUP, (c + 1) * GROUP)
                     banks = []
-                    for name in ("w1", "w3"):
+                    for name in ("w3", "w1"):
                         pool = psum_1 if name == "w1" else psum_3
-                        bank = pool.tile([P, PACK * GROUP], F32, name=f"{name}_bank")
+                        bank = pool.tile([P, PACK * GROUP], F32, name=f"{name}_bank", tag=f"{name}_bank")
                         for t in range(PACK):
                             m_cols = slice(t * P, (t + 1) * P)
                             nc.tensor.matmul_mx(
@@ -198,38 +200,18 @@ def tile_picked_pick_glu_sigmoid_sub_e_kernel(tc, xT, w1, w3, w2, offs, out):
                             )
                         banks.append(bank)
                     gate = work.tile([P, GROUP * PACK], F32, name="gate")
-                    nc.scalar.activation(
-                        gate[:].rearrange("p (n t) -> p n t", t=PACK),
-                        banks[0][:].rearrange("p (t n) -> p n t", t=PACK),
-                        Sigmoid,
-                    )
+                    nc.scalar.activation(gate[:], banks[1][:], Sigmoid)
                     into = hidden[:, c * GROUP * PACK : (c + 1) * GROUP * PACK]
-                    if (h, s, c) in ON_GPSIMD:
-                        value = work.tile([P, GROUP * PACK], F32, name="value")
-                        nc.scalar.activation(
-                            value[:].rearrange("p (n t) -> p n t", t=PACK),
-                            banks[1][:].rearrange("p (t n) -> p n t", t=PACK),
-                            Copy,
-                        )
-                        for a in (0, 256):
-                            nc.gpsimd.tensor_tensor(into[:, a : a + 256], value[:, a : a + 256], gate[:, a : a + 256], mult)
-                    else:
-                        nc.vector.tensor_tensor(
-                            into.rearrange("p (n t) -> p n t", t=PACK),
-                            banks[1][:].rearrange("p (t n) -> p n t", t=PACK),
-                            gate[:].rearrange("p (n t) -> p n t", t=PACK),
-                            mult,
-                        )
-                        for job in pending:
-                            job()
-                        pending.clear()
-                    if (h, s, c) == (0, 0, 0):
-                        gather(1, 1)
-                    if (h, s, c) == (0, 0, 1):
-                        gather(1, 2)
-                        quantize_x(1)
+                    nc.vector.tensor_tensor(
+                        into.rearrange("p (n t) -> p n t", t=PACK),
+                        banks[0][:].rearrange("p (t n) -> p n t", t=PACK),
+                        gate[:].rearrange("p (t n) -> p n t", t=PACK),
+                        mult,
+                    )
+                    for job in pending:
+                        job()
+                    pending.clear()
                     if (h, s, c) == (0, 0, 2):
-                        quantize_x(2)
                         load_b()
                     if (h, s, c) == (0, 2, 0):
                         quantize_w("w1", 1, later[0])

@@ -22,6 +22,7 @@ add = mybir.AluOpType.add
 CHUNK = 1024
 SLICE = 512
 GROUP = 128
+RUN = 2
 HALF = 512
 
 
@@ -88,9 +89,10 @@ def tile_picked_pick_glu_sigmoid_sub_e_kernel(tc, xT, w1, w3, w2, offs, out):
             rows = w.rearrange("(p j) c -> p j c", j=PACK)
             nc.sync.dma_start(out=raw[:], in_=rows[:, :, h * HALF : (h + 1) * HALF])
             grouped = keep.tile([P, HALF * PACK], BF16, align_bytes=64, name=f"{name}_grouped{h}")
-            src = raw[:].rearrange("p j (q t r) -> p t q r j", t=PACK, r=8)
-            dst = grouped[:].rearrange("p (t q r j) -> p t q r j", t=PACK, r=8, j=PACK)
             for t, engine in enumerate(engines):
+                order = "p t q r j" if engine == "G" else "p t q j r"
+                src = raw[:].rearrange("p j (q t r) -> " + order, t=PACK, r=RUN)
+                dst = grouped[:].rearrange("p (t q r j) -> " + order, t=PACK, r=RUN, j=PACK)
                 if engine == "S":
                     nc.scalar.activation(dst[:, t], src[:, t], Copy)
                 elif engine == "V":
@@ -114,8 +116,8 @@ def tile_picked_pick_glu_sigmoid_sub_e_kernel(tc, xT, w1, w3, w2, offs, out):
         quantize_x(0)
         gather(1, 2)
         quantize_x(1)
-        w3a = load_w("w3", w3, 0, "SGSG")
-        w1a = load_w("w1", w1, 0, "SGSG")
+        w3a = load_w("w3", w3, 0, "SSSS")
+        w1a = load_w("w1", w1, 0, "SSVS")
         quantize_w("w3", 0, w3a)
         quantize_x(2)
         quantize_w("w1", 0, w1a)
@@ -130,7 +132,7 @@ def tile_picked_pick_glu_sigmoid_sub_e_kernel(tc, xT, w1, w3, w2, offs, out):
         w2_grouped = keep.tile([P, halves * N * PACK], BF16, align_bytes=64, name="w2_grouped")
         w2_codes = keep.tile([P, halves * N], U32, align_bytes=64, name="w2_codes")
         w2_scales = keep.tile([P, halves * N], U8, align_bytes=64, name="w2_scales")
-        w2_rows = w2.rearrange("(g q t r) m -> g t q r m", g=halves, t=PACK, r=8)
+        w2_rows = w2.rearrange("(g q t r) m -> g t q r m", g=halves, t=PACK, r=RUN)
 
         def load_w2():
             for g in range(halves):
@@ -200,12 +202,17 @@ def tile_picked_pick_glu_sigmoid_sub_e_kernel(tc, xT, w1, w3, w2, offs, out):
                             )
                         banks.append(bank)
                     gate = work.tile([P, GROUP * PACK], F32, name="gate")
-                    nc.scalar.activation(gate[:], banks[1][:], Sigmoid)
+                    in_quads = "p (t c i) -> p c t i"
+                    nc.scalar.activation(
+                        gate[:].rearrange("p (c t i) -> p c t i", t=PACK, i=RUN),
+                        banks[1][:].rearrange(in_quads, t=PACK, i=RUN),
+                        Sigmoid,
+                    )
                     into = hidden[:, c * GROUP * PACK : (c + 1) * GROUP * PACK]
                     nc.vector.tensor_tensor(
-                        into.rearrange("p (n t) -> p n t", t=PACK),
-                        banks[0][:].rearrange("p (t n) -> p n t", t=PACK),
-                        gate[:].rearrange("p (t n) -> p n t", t=PACK),
+                        into.rearrange("p (c i t) -> p c t i", t=PACK, i=RUN),
+                        gate[:].rearrange("p (c t i) -> p c t i", t=PACK, i=RUN),
+                        banks[0][:].rearrange(in_quads, t=PACK, i=RUN),
                         mult,
                     )
                     for job in pending:

from contextlib import ExitStack
from functools import partial

import concourse.mybir as mybir

K, T, S, H, N = 512, 4096, 1536, 1024, 128
FLOPS = 2 * S * (2 * K * H + H * N)

P = 128
PACK = 4
F32 = mybir.dt.float32
BF16 = mybir.dt.bfloat16
U32 = mybir.dt.uint32
U16 = mybir.dt.uint16
U8 = mybir.dt.uint8
FP8X4 = mybir.dt.float8_e4m3fn_x4
Copy = mybir.ActivationFunctionType.Copy
Sigmoid = mybir.ActivationFunctionType.Sigmoid
mult = mybir.AluOpType.mult
add = mybir.AluOpType.add

CHUNK = 1024
SLICE = 512
GROUP = 128
RUN = 2
HALF = 512


def tile_picked_pick_glu_sigmoid_sub_e_kernel(tc, xT, w1, w3, w2, offs, out):
    nc = tc.nc
    slices = S // SLICE
    halves = H // HALF
    with ExitStack() as ctx:
        keep = ctx.enter_context(tc.tile_pool(name="keep", bufs=1))
        stage = ctx.enter_context(tc.tile_pool(name="stage", bufs=8))
        work = ctx.enter_context(tc.tile_pool(name="work", bufs=4))
        res = ctx.enter_context(tc.tile_pool(name="res", bufs=3))
        psum_1 = ctx.enter_context(tc.psum_pool(name="psum_1", bufs=4))
        psum_3 = ctx.enter_context(tc.psum_pool(name="psum_3", bufs=4))

        offsets = keep.tile([P, S // 16], U16, name="offsets")
        nc.sync.dma_start(offsets[:], offs)

        warm = keep.tile([P, 8], F32, name="warm")
        nc.vector.memset(warm[:], 0.0)
        nc.scalar.activation(warm[:, 0:1], warm[:, 0:1], Sigmoid)

        x_rows = xT.rearrange("(p j) t -> p j t", j=PACK)
        pairs = [keep.tile([P, 2 * T], BF16, align_bytes=64, name=f"pairs{u}") for u in range(2)]
        picked = [keep.tile([P, SLICE * PACK], BF16, align_bytes=64, name=f"picked{s}") for s in range(slices)]
        x_codes = [keep.tile([P, SLICE], U32, align_bytes=64, name=f"x_codes{s}") for s in range(slices)]
        x_scales = [keep.tile([P, SLICE], U8, align_bytes=64, name=f"x_scales{s}") for s in range(slices)]

        def load_x(u, t0, width, engines):
            raw = stage.tile([P, 2, width], F32, name="raw")
            nc.sync.dma_start(out=raw[:], in_=x_rows[:, 2 * u : 2 * u + 2, t0 : t0 + width])
            part = width // len(engines)
            for i, engine in enumerate(engines):
                a = t0 + i * part
                dst = pairs[u][:, 2 * a : 2 * (a + part)].rearrange("p (t e) -> p t e", e=2)
                src = raw[:, :, i * part : (i + 1) * part].rearrange("p e t -> p t e")
                if engine == "V":
                    nc.vector.tensor_copy(dst, src)
                else:
                    nc.scalar.activation(dst, src, Copy)

        def gather(u, s):
            words = picked[s][:].bitcast(U32).rearrange("p (n u) -> p n u", u=2)
            window = pairs[u][:].bitcast(U32)
            cols = offsets[:, s * (SLICE // 16) : (s + 1) * (SLICE // 16)]
            nc.vector.tensor_copy(words[:, :, u], window.indirect(cols))

        for i in range(4):
            load_x(0, i * CHUNK, CHUNK, "SV"[i % 2])
        load_x(1, 0, CHUNK, "S")
        gather(0, 0)
        load_x(1, CHUNK, CHUNK, "V")
        gather(0, 1)
        load_x(1, 2 * CHUNK, CHUNK, "S")
        gather(0, 2)
        load_x(1, 3 * CHUNK, CHUNK // 2, "VS")
        load_x(1, 3 * CHUNK + CHUNK // 2, CHUNK // 2, "V")

        w_codes = {}
        w_scales = {}

        def load_w(name, w, h, engines):
            raw = stage.tile([P, PACK, HALF], F32, name="raw")
            rows = w.rearrange("(p j) c -> p j c", j=PACK)
            nc.sync.dma_start(out=raw[:], in_=rows[:, :, h * HALF : (h + 1) * HALF])
            grouped = keep.tile([P, HALF * PACK], BF16, align_bytes=64, name=f"{name}_grouped{h}")
            for t, engine in enumerate(engines):
                order = "p t q r j" if engine == "G" else "p t q j r"
                src = raw[:].rearrange("p j (q t r) -> " + order, t=PACK, r=RUN)
                dst = grouped[:].rearrange("p (t q r j) -> " + order, t=PACK, r=RUN, j=PACK)
                if engine == "S":
                    nc.scalar.activation(dst[:, t], src[:, t], Copy)
                elif engine == "V":
                    nc.vector.tensor_copy(dst[:, t], src[:, t])
                else:
                    nc.gpsimd.tensor_scalar(dst[:, t], src[:, t], 1.0, 0.0, mult, add)
            return grouped

        def quantize_w(name, h, grouped):
            codes = keep.tile([P, HALF], U32, align_bytes=64, name=f"{name}_codes{h}")
            scales = keep.tile([P, HALF], U8, align_bytes=64, name=f"{name}_scales{h}")
            nc.vector.quantize_mx(out=codes[:].bitcast(FP8X4), scales=scales[:], in_=grouped[:])
            w_codes[name, h] = codes
            w_scales[name, h] = scales

        def quantize_x(s):
            nc.vector.quantize_mx(out=x_codes[s][:].bitcast(FP8X4), scales=x_scales[s][:], in_=picked[s][:])

        gather(1, 0)
        gather(1, 1)
        quantize_x(0)
        gather(1, 2)
        quantize_x(1)
        w3a = load_w("w3", w3, 0, "SSSS")
        w1a = load_w("w1", w1, 0, "SSVS")
        quantize_w("w3", 0, w3a)
        quantize_x(2)
        quantize_w("w1", 0, w1a)

        later = []

        def load_b():
            later.append(load_w("w1", w1, 1, "GGGG"))
            later.append(load_w("w3", w3, 1, "GGGG"))

        w2_raw = keep.tile([P, halves, PACK, N], F32, name="w2_raw")
        w2_grouped = keep.tile([P, halves * N * PACK], BF16, align_bytes=64, name="w2_grouped")
        w2_codes = keep.tile([P, halves * N], U32, align_bytes=64, name="w2_codes")
        w2_scales = keep.tile([P, halves * N], U8, align_bytes=64, name="w2_scales")
        w2_rows = w2.rearrange("(g q t r) m -> g t q r m", g=halves, t=PACK, r=RUN)

        def load_w2():
            for g in range(halves):
                for t in range(PACK):
                    nc.sync.dma_start(out=w2_raw[:, g, t, :], in_=w2_rows[g, t])
            for g in range(halves):
                nc.gpsimd.tensor_scalar(
                    w2_grouped[:, g * N * PACK : (g + 1) * N * PACK].rearrange("p (m t) -> p m t", t=PACK),
                    w2_raw[:, g].rearrange("p t m -> p m t"),
                    1.0, 0.0, mult, add,
                )
            nc.vector.quantize_mx(out=w2_codes[:].bitcast(FP8X4), scales=w2_scales[:], in_=w2_grouped[:])

        h_codes = {}
        h_scales = {}
        pending = []

        def finish(h, s, hidden, start, done):
            n_cols = slice(start, done)
            nc.vector.quantize_mx(
                out=h_codes[h, s][:, n_cols].bitcast(FP8X4),
                scales=h_scales[h, s][:, n_cols],
                in_=hidden[:, start * PACK : done * PACK],
            )
            if h < halves - 1:
                return
            acc = psum_1.tile([P, done - start], F32, name="acc", tag="w1_bank")
            for g in range(halves):
                nc.tensor.matmul_mx(
                    out=acc[:],
                    lhsT=w2_codes[:, g * N : (g + 1) * N].bitcast(FP8X4),
                    lhsT_scale=w2_scales[:, g * N : (g + 1) * N],
                    rhs=h_codes[g, s][:, n_cols].bitcast(FP8X4),
                    rhs_scale=h_scales[g, s][:, n_cols],
                    start=(g == 0),
                    stop=(g == halves - 1),
                )
            y = res.tile([P, done - start], F32, name="y")
            nc.scalar.copy(y[:], acc[:])
            nc.sync.dma_start(out=out[:, s * SLICE + start : s * SLICE + done], in_=y[:])

        for h in range(halves):
            for s in range(slices):
                hidden = work.tile([P, SLICE * PACK], BF16, align_bytes=64, name="hidden")
                codes = keep.tile([P, SLICE], U32, align_bytes=64, name=f"h_codes{h}_{s}")
                scales = keep.tile([P, SLICE], U8, align_bytes=64, name=f"h_scales{h}_{s}")
                h_codes[h, s] = codes
                h_scales[h, s] = scales
                last = h == halves - 1 and s == slices - 1
                ends = [256, 512] if last else [SLICE]
                for c in range(SLICE // GROUP):
                    n_cols = slice(c * GROUP, (c + 1) * GROUP)
                    banks = []
                    for name in ("w3", "w1"):
                        pool = psum_1 if name == "w1" else psum_3
                        bank = pool.tile([P, PACK * GROUP], F32, name=f"{name}_bank", tag=f"{name}_bank")
                        for t in range(PACK):
                            m_cols = slice(t * P, (t + 1) * P)
                            nc.tensor.matmul_mx(
                                out=bank[:, t * GROUP : (t + 1) * GROUP],
                                lhsT=w_codes[name, h][:, m_cols].bitcast(FP8X4),
                                lhsT_scale=w_scales[name, h][:, m_cols],
                                rhs=x_codes[s][:, n_cols].bitcast(FP8X4),
                                rhs_scale=x_scales[s][:, n_cols],
                                start=True,
                                stop=True,
                            )
                        banks.append(bank)
                    gate = work.tile([P, GROUP * PACK], F32, name="gate")
                    in_quads = "p (t c i) -> p c t i"
                    nc.scalar.activation(
                        gate[:].rearrange("p (c t i) -> p c t i", t=PACK, i=RUN),
                        banks[1][:].rearrange(in_quads, t=PACK, i=RUN),
                        Sigmoid,
                    )
                    into = hidden[:, c * GROUP * PACK : (c + 1) * GROUP * PACK]
                    nc.vector.tensor_tensor(
                        into.rearrange("p (c i t) -> p c t i", t=PACK, i=RUN),
                        gate[:].rearrange("p (c t i) -> p c t i", t=PACK, i=RUN),
                        banks[0][:].rearrange(in_quads, t=PACK, i=RUN),
                        mult,
                    )
                    for job in pending:
                        job()
                    pending.clear()
                    if (h, s, c) == (0, 0, 2):
                        load_b()
                    if (h, s, c) == (0, 2, 0):
                        quantize_w("w1", 1, later[0])
                    if (h, s, c) == (0, 2, 2):
                        quantize_w("w3", 1, later[1])
                        load_w2()
                    done = (c + 1) * GROUP
                    if done in ends:
                        start = ([0] + ends)[ends.index(done)]
                        pending.append(partial(finish, h, s, hidden, start, done))
        for job in pending:
            job()
